import numpy as np
import ml_dtypes


def mxq(x, axis, fmt="e4m3"):
    dtype, down = {"e4m3": (ml_dtypes.float8_e4m3fn, 7), "e5m2": (ml_dtypes.float8_e5m2, 14)}[fmt]
    v = np.moveaxis(np.asarray(x, np.float32).astype(ml_dtypes.bfloat16).astype(np.float64), axis, -1)
    blocks = v.reshape(v.shape[:-1] + (-1, 32))
    amax = np.abs(blocks).max(-1, keepdims=True)
    byte = np.maximum(np.where(amax > 0, np.frexp(amax)[1] - 1 + 127, 0) - down, 1)
    scale = np.exp2(byte - 127.0)
    codes = (blocks / scale).astype(np.float32).astype(dtype).astype(np.float64)
    return np.moveaxis((codes * scale).reshape(v.shape), -1, axis)


WIDE = False


def mx_kscale(k):
    if not WIDE:
        return np.ones(k)
    levels = np.array([10, -10, 5, -5, 0])
    if k % 512:
        return np.exp2(np.random.permutation(np.resize(levels, k // 32))).repeat(32)
    a = np.empty((k // 512, 16))
    for p in range(k // 512):
        a[p, :8] = np.random.permutation(np.resize(levels, 8))
        for g in range(8):
            far = levels[np.abs(levels - a[p, g]) >= 10]
            a[p, g + 8] = far[np.random.randint(len(far))]
    return np.exp2(a.ravel()).repeat(32)


def f64(x):
    return np.asarray(x).astype(np.float64)


def striped(idx):
    return np.tile(idx.reshape(-1, 16).T, (8, 1)).astype(np.uint16)


def unstriped(offs):
    return offs[:16].T.reshape(-1).astype(np.int64)


def striped8(idx):
    return np.concatenate([x.reshape(-1, 16).T for x in idx]).astype(np.uint16)


def runs(offs, k):
    lists = np.stack([offs[16 * r : 16 * r + 16].T.reshape(-1) for r in range(8)]).astype(np.int64)
    return lists[np.arange(k) % 512 // 64]


def pack_weight(w):
    k, n = w.shape
    w = f64(np.asarray(w, np.float32).astype(ml_dtypes.bfloat16)).reshape(k // 32, 32, n)
    amax = np.abs(w).max(1)
    byte = np.clip(np.where(amax > 0, np.frexp(amax)[1] - 1 + 127 - 7, 1), 1, 254)
    scaled = (w * np.exp2(127.0 - byte)[:, None, :]).reshape(k, n).astype(np.float32)
    words = np.ascontiguousarray(scaled.reshape(k // 512, 128, 4, n).transpose(0, 1, 3, 2)).astype(ml_dtypes.float8_e4m3fn).view(np.uint8)
    return words, np.ascontiguousarray(byte.astype(np.uint8).reshape(k // 512, 16, n))


def unpack_weight(words, scales):
    g, p, n, _ = words.shape
    vals = np.ascontiguousarray(words).view(ml_dtypes.float8_e4m3fn).astype(np.float64) * np.repeat(np.exp2(scales.astype(np.float64) - 127.0), 8, axis=1)[..., None]
    return vals.transpose(0, 1, 3, 2).reshape(g * 512, n)


def sigmoid(v):
    return 1.0 / (1.0 + np.exp(-np.maximum(v, -700.0)))


K, T, S, N, H, G, W = 512, 2048, 512, 512, 512, 2048, 256


def setup_inputs():
    n = np.random.standard_normal
    s = mx_kscale(K)[:, None]
    u = mx_kscale(S)
    packed_xT = pack_weight(n((K, T)) * s)
    packed_dT = pack_weight(n((K, G)) / s)
    perm = np.stack([np.random.permutation(S) for _ in range(8)])
    return {
        "x_words": packed_xT[0],
        "x_scales": packed_xT[1],
        "w1": (n((K, H)) / np.sqrt(K) / s).astype(np.float32),
        "d_words": packed_dT[0],
        "d_scales": packed_dT[1],
        "gn": (np.random.uniform(0.5, 1.5, (H, 1)) * u[:, None]).astype(np.float32),
        "w2": (n((H, N)) / np.sqrt(H) / u[:, None]).astype(np.float32),
        "offs": striped(np.random.permutation(T)[:S]),
        "k1": striped8(np.random.randint(0, G, (8, H))),
        "two": striped(np.random.permutation(T)[:S]),
        "n1": striped(np.random.permutation(S)),
        "n2": striped(np.random.permutation(S)),
        "n3": striped8(perm[:, :W]),
        "n4": striped8(perm[:, W:]),
    }


def reference(x_words, x_scales, w1, d_words, d_scales, gn, w2, offs, k1, two, n1, n2, n3, n4):
    xq = unpack_weight(x_words, x_scales)[:, unstriped(offs)]
    y = mxq(f64(w1), 0, "e4m3").T @ xq
    d_k1 = unpack_weight(d_words, d_scales)[np.arange(K)[:, None], runs(k1, K)]
    x_two = unpack_weight(x_words, x_scales)[:, unstriped(two)]
    d = 0.0625 * (d_k1.T @ x_two)
    z = f64(gn) * (y[:, unstriped(n1)] - (np.tanh(d) * d[:, unstriped(n2)]))
    h = mxq(f64(w2), 0, "e4m3").T @ mxq(z, 0, "e4m3")
    pb = h[np.arange(N)[:, None], runs(n4, N)]
    pa = h[np.arange(N)[:, None], runs(n3, N)]
    rb = pb * sigmoid(pb - pa)
    ra = pa * sigmoid(pa - pb)
    ds = np.zeros((N, S))
    ds[np.arange(N)[:, None], runs(n3, N)] = ra
    out = ds.copy()
    out[np.arange(N)[:, None], runs(n4, N)] = rb
    return out

@@ -1,0 +1,233 @@
+from contextlib import ExitStack
+
+import concourse.mybir as mybir
+
+K, T, S, N, H, G, W = 512, 2048, 512, 512, 512, 2048, 256
+FLOPS = 2 * K * H * S * 2 + 2 * H * N * S
+
+F32 = mybir.dt.float32
+BF16 = mybir.dt.bfloat16
+I32 = mybir.dt.int32
+U32 = mybir.dt.uint32
+U16 = mybir.dt.uint16
+U8 = mybir.dt.uint8
+FP8X4 = mybir.dt.float8_e4m3fn_x4
+ALU = mybir.AluOpType
+ACT = mybir.ActivationFunctionType
+
+P = 128
+PACK = 4
+HALF = S // 2
+
+
+def tile_picked_twkeysoftbduel_none_p_kernel(
+    tc, x_words, x_scales, w1, d_words, d_scales, gn, w2, offs, k1, two, n1, n2, n3, n4, out
+):
+    nc = tc.nc
+    with ExitStack() as ctx:
+        sb = ctx.enter_context(tc.tile_pool(name="sb", bufs=1))
+        ps = ctx.enter_context(tc.psum_pool(name="ps", bufs=1))
+
+        def tile(name, shape, dtype):
+            return sb.tile(shape, dtype, name=name, align_bytes=64)
+
+        def bank(b, width):
+            return ps.tile([P, width], F32, name="bank%d" % b)
+
+        def load_list(name, src):
+            t = sb.tile(list(src.shape), U16, name=name)
+            nc.sync.dma_start(t[:], src)
+            return t
+
+        def as_words(dram):
+            return dram[0].rearrange("p n r -> p (n r)").bitcast(I32)
+
+        def mx(acc, lhs_codes, lhs_scales, rhs_codes, rhs_scales):
+            nc.tensor.matmul_mx(
+                out=acc,
+                lhsT=lhs_codes.bitcast(FP8X4),
+                lhsT_scale=lhs_scales,
+                rhs=rhs_codes.bitcast(FP8X4),
+                rhs_scale=rhs_scales,
+                start=True,
+                stop=True,
+            )
+
+        xs_table = tile("xs_table", [P, T], U8)
+        ds_table = tile("ds_table", [P, G], U8)
+        ds_moved = tile("ds_moved", [P, H], U8)
+        nc.gpsimd.memset(ds_table[:].bitcast(I32), 0)
+        nc.vector.memset(xs_table[:].bitcast(I32), 0)
+        nc.gpsimd.memset(ds_moved[:].bitcast(I32), 0)
+
+        k1_l = load_list("k1_l", k1)
+        w1_raw = [tile("w1_raw%d" % u, [P, PACK, H // 2], F32) for u in range(2)]
+        w1_view = w1.rearrange("(p j) c -> p j c", j=PACK)
+        nc.sync.dma_start(out=w1_raw[0][:], in_=w1_view[:, :, : H // 2])
+        nc.sync.dma_start(out=ds_table[:].bitcast(I32)[0:P:8, :], in_=d_scales[0].bitcast(I32))
+        for q in range(4):
+            nc.sync.dma_start(
+                out=xs_table[:].bitcast(I32)[32 * q : 32 * q + 4, :],
+                in_=x_scales[0].bitcast(I32)[4 * q : 4 * q + 4, :],
+            )
+        offs_l = load_list("offs_l", offs)
+        nc.sync.dma_start(out=w1_raw[1][:], in_=w1_view[:, :, H // 2 :])
+        two_l = load_list("two_l", two)
+        xw_table = tile("xw_table", [P, T], U32)
+        nc.sync.dma_start(out=xw_table[:].bitcast(I32), in_=as_words(x_words))
+        dw_table = tile("dw_table", [P, G], U32)
+        nc.sync.dma_start(out=dw_table[:].bitcast(I32), in_=as_words(d_words))
+        gain = tile("gain", [P, PACK], F32)
+        nc.sync.dma_start(out=gain[:], in_=gn.rearrange("(p t) o -> p (t o)", t=PACK))
+        n1_l = load_list("n1_l", n1)
+        n2_l = load_list("n2_l", n2)
+        w2_raw = tile("w2_raw", [P, PACK, N], F32)
+        nc.sync.dma_start(out=w2_raw[:], in_=w2.rearrange("(p j) c -> p j c", j=PACK))
+        n3_l = load_list("n3_l", n3)
+        n4_l = load_list("n4_l", n4)
+
+        ds_picked = tile("ds_picked", [P, H], U8)
+        nc.vector.tensor_copy(out=ds_picked[:], in_=ds_table[:].indirect(k1_l[:]))
+        for q in range(4):
+            nc.scalar.dma_start(
+                out=ds_moved[:].bitcast(I32)[32 * q : 32 * q + 4, :],
+                in_=ds_picked[:].bitcast(I32)[32 * q : 32 * q + 32 : 8, :],
+            )
+        xs_offs = tile("xs_offs", [P, S], U8)
+        nc.vector.tensor_copy(out=xs_offs[:], in_=xs_table[:].indirect(offs_l[:]))
+        xs_two = tile("xs_two", [P, S], U8)
+        nc.vector.tensor_copy(out=xs_two[:], in_=xs_table[:].indirect(two_l[:]))
+
+        w1_bf = tile("w1_bf", [P, PACK, P, PACK], BF16)
+        for u in range(2):
+            nc.scalar.copy(
+                out=w1_bf[:].rearrange("p t m j -> p m j t")[:, u * (P // 2) : (u + 1) * (P // 2)],
+                in_=w1_raw[u][:].rearrange("p j (m t) -> p m j t", t=PACK),
+            )
+        xw_offs = tile("xw_offs", [P, S], U32)
+        nc.vector.tensor_copy(out=xw_offs[:], in_=xw_table[:].indirect(offs_l[:]))
+        w1_codes = tile("w1_codes", [P, H], U32)
+        w1_scales = tile("w1_scales", [P, H], U8)
+        nc.vector.quantize_mx(
+            out=w1_codes[:].bitcast(FP8X4), scales=w1_scales[:], in_=w1_bf[:].rearrange("p t m j -> p (t m j)")
+        )
+        y_ps = [bank(t, S) for t in range(PACK)]
+        for t in range(PACK):
+            cols = slice(t * P, (t + 1) * P)
+            mx(y_ps[t][:], w1_codes[:, cols], w1_scales[:, cols], xw_offs[:], xs_offs[:])
+
+        xw_two = tile("xw_two", [P, S], U32)
+        nc.vector.tensor_copy(out=xw_two[:], in_=xw_table[:].indirect(two_l[:]))
+        dw_picked = tile("dw_picked", [P, H], U32)
+        nc.vector.tensor_copy(out=dw_picked[:], in_=dw_table[:].indirect(k1_l[:]))
+        ds_dealt = tile("ds_dealt", [P, H], U8)
+        nc.vector.tensor_copy(
+            out=ds_dealt[:].rearrange("p (t m) -> p t m", t=PACK),
+            in_=ds_moved[:].rearrange("p (m t) -> p t m", t=PACK),
+        )
+        dw_dealt = tile("dw_dealt", [P, H], U32)
+        nc.vector.tensor_copy(
+            out=dw_dealt[:].rearrange("p (t m) -> p m t", t=PACK),
+            in_=dw_picked[:].rearrange("p (m t) -> p m t", t=PACK),
+        )
+        d_ps = [bank(PACK + t, S) for t in range(PACK)]
+        for t in range(PACK):
+            cols = slice(t * P, (t + 1) * P)
+            mx(d_ps[t][:], dw_dealt[:, cols], ds_dealt[:, cols], xw_two[:], xs_two[:])
+
+        y_rows = [tile("y_rows%d" % t, [P, S], F32) for t in range(PACK)]
+        d_rows = [tile("d_rows%d" % t, [P, S], F32) for t in range(PACK)]
+        d_tanh = [tile("d_tanh%d" % t, [P, S], F32) for t in range(PACK)]
+        for t in range(PACK):
+            nc.scalar.activation(out=y_rows[t][:], in_=y_ps[t][:], func=ACT.Copy, scale=gain[:, t : t + 1])
+        for t in range(PACK):
+            nc.vector.tensor_scalar(
+                out=d_rows[t][:],
+                in0=d_ps[t][:],
+                scalar1=gain[:, t : t + 1],
+                scalar2=0.0625,
+                op0=ALU.mult,
+                op1=ALU.mult,
+            )
+            nc.scalar.activation(out=d_tanh[t][:], in_=d_ps[t][:], func=ACT.Tanh, scale=0.0625)
+
+        lc = HALF // 16
+        y_at = [tile("y_at%d" % u, [P, PACK, HALF], F32) for u in range(2)]
+        prod = [tile("prod%d" % u, [P, PACK, HALF], F32) for u in range(2)]
+        for u in range(2):
+            for t in range(PACK):
+                nc.scalar.activation(
+                    out=y_at[u][:, t, :], in_=y_rows[t][:].indirect(n1_l[:, u * lc : (u + 1) * lc]), func=ACT.Copy
+                )
+        for u in range(2):
+            for t in range(PACK):
+                nc.vector.tensor_tensor(
+                    out=prod[u][:, t, :],
+                    in0=d_rows[t][:].indirect(n2_l[:, u * lc : (u + 1) * lc]),
+                    in1=d_tanh[t][:, u * HALF : (u + 1) * HALF],
+                    op=ALU.mult,
+                )
+
+        w2_bf = [tile("w2_bf%d" % v, [P, 2, P, PACK], BF16) for v in range(2)]
+        w2_codes = [tile("w2_codes%d" % v, [P, 2 * P], U32) for v in range(2)]
+        w2_scales = [tile("w2_scales%d" % v, [P, 2 * P], U8) for v in range(2)]
+        z_bf = [tile("z_bf%d" % u, [P, HALF, PACK], BF16) for u in range(2)]
+        z_codes = [tile("z_codes%d" % u, [P, HALF], U32) for u in range(2)]
+        z_scales = [tile("z_scales%d" % u, [P, HALF], U8) for u in range(2)]
+        for u in range(2):
+            nc.scalar.copy(
+                out=w2_bf[u][:].rearrange("p e m j -> p m j e"),
+                in_=w2_raw[:].rearrange("p j (m t) -> p m j t", t=PACK)[:, :, :, 2 * u : 2 * u + 2],
+            )
+            nc.vector.tensor_tensor(
+                out=z_bf[u][:].rearrange("p (c i) t -> p c t i", i=4),
+                in0=y_at[u][:].rearrange("p t (c i) -> p c t i", i=4),
+                in1=prod[u][:].rearrange("p t (c i) -> p c t i", i=4),
+                op=ALU.subtract,
+            )
+            nc.vector.quantize_mx(
+                out=z_codes[u][:].bitcast(FP8X4), scales=z_scales[u][:], in_=z_bf[u][:].rearrange("p c t -> p (c t)")
+            )
+            nc.vector.quantize_mx(
+                out=w2_codes[u][:].bitcast(FP8X4),
+                scales=w2_scales[u][:],
+                in_=w2_bf[u][:].rearrange("p e m j -> p (e m j)"),
+            )
+
+        h_ps = {}
+        for v in range(2):
+            for u in range(2):
+                for e in range(2):
+                    t = 2 * v + e
+                    h_ps[t, u] = bank(PACK * u + t, HALF)
+                    cols = slice(e * P, (e + 1) * P)
+                    mx(h_ps[t, u][:], w2_codes[v][:, cols], w2_scales[v][:, cols], z_codes[u][:], z_scales[u][:])
+
+        out_rows = out.rearrange("(p t) c -> t p c", t=PACK)
+        h_rows = [tile("h_rows%d" % t, [P, S], F32) for t in range(PACK)]
+        pa = [tile("pa%d" % t, [P, W], F32) for t in range(PACK)]
+        pb = [tile("pb%d" % t, [P, W], F32) for t in range(PACK)]
+        diff = [tile("diff%d" % t, [P, W], F32) for t in range(PACK)]
+        sig_a = [tile("sig_a%d" % t, [P, W], F32) for t in range(PACK)]
+        sig_b = [tile("sig_b%d" % t, [P, W], F32) for t in range(PACK)]
+        res = [tile("res%d" % t, [P, S], F32) for t in range(PACK)]
+
+        def fetch_pairs(t):
+            for u in range(2):
+                nc.scalar.copy(out=h_rows[t][:, u * HALF : (u + 1) * HALF], in_=h_ps[t, u][:])
+            if t == 0:
+                nc.vector.tensor_copy(out=pa[t][:], in_=h_rows[t][:].indirect(n3_l[:]))
+            else:
+                nc.scalar.activation(out=pa[t][:], in_=h_rows[t][:].indirect(n3_l[:]), func=ACT.Copy)
+            nc.scalar.activation(out=pb[t][:], in_=h_rows[t][:].indirect(n4_l[:]), func=ACT.Copy)
+            nc.vector.tensor_tensor(out=diff[t][:], in0=pa[t][:], in1=pb[t][:], op=ALU.subtract)
+
+        fetch_pairs(0)
+        for t in range(PACK):
+            nc.scalar.activation(out=sig_a[t][:], in_=diff[t][:], func=ACT.Sigmoid)
+            nc.vector.tensor_tensor(out=res[t][:].indirect(n3_l[:]), in0=pa[t][:], in1=sig_a[t][:], op=ALU.mult)
+            if t + 1 < PACK:
+                fetch_pairs(t + 1)
+            nc.scalar.activation(out=sig_b[t][:], in_=diff[t][:], func=ACT.Sigmoid, scale=-1.0)
+            nc.vector.tensor_tensor(out=res[t][:].indirect(n4_l[:]), in0=pb[t][:], in1=sig_b[t][:], op=ALU.mult)
+            nc.sync.dma_start(out=out_rows[t], in_=res[t][:])

@@ -26,10 +26,14 @@ def tile_picked_twkeysoftbduel_none_p_kernel(
     nc = tc.nc
     with ExitStack() as ctx:
         sb = ctx.enter_context(tc.tile_pool(name="sb", bufs=1))
+        shared = ctx.enter_context(tc.tile_pool(name="shared", bufs=1))
         ps = ctx.enter_context(tc.psum_pool(name="ps", bufs=1))
 
         def tile(name, shape, dtype):
             return sb.tile(shape, dtype, name=name, align_bytes=64)
+
+        def placed(name, shape, dtype, offset):
+            return shared.tile(shape, dtype, name=name, align_bytes=64, offset=offset)
 
         def bank(b, width):
             return ps.tile([P, width], F32, name="bank%d" % b)
@@ -56,71 +60,76 @@ def tile_picked_twkeysoftbduel_none_p_kernel(
         xs_table = tile("xs_table", [P, T], U8)
         ds_table = tile("ds_table", [P, G], U8)
         ds_moved = tile("ds_moved", [P, H], U8)
-        nc.gpsimd.memset(ds_table[:].bitcast(I32), 0)
-        nc.vector.memset(xs_table[:].bitcast(I32), 0)
+        nc.gpsimd.memset(xs_table[:].bitcast(I32), 0)
+        nc.vector.memset(ds_table[:].bitcast(I32), 0)
+        warm = tile("warm", [P, 2], F32)
+        nc.vector.memset(warm[:, 0:1], 0.0)
         nc.gpsimd.memset(ds_moved[:].bitcast(I32), 0)
 
+        offs_l = load_list("offs_l", offs)
         k1_l = load_list("k1_l", k1)
-        w1_raw = [tile("w1_raw%d" % u, [P, PACK, H // 2], F32) for u in range(2)]
-        w1_view = w1.rearrange("(p j) c -> p j c", j=PACK)
-        nc.sync.dma_start(out=w1_raw[0][:], in_=w1_view[:, :, : H // 2])
-        nc.sync.dma_start(out=ds_table[:].bitcast(I32)[0:P:8, :], in_=d_scales[0].bitcast(I32))
         for q in range(4):
             nc.sync.dma_start(
                 out=xs_table[:].bitcast(I32)[32 * q : 32 * q + 4, :],
                 in_=x_scales[0].bitcast(I32)[4 * q : 4 * q + 4, :],
             )
-        offs_l = load_list("offs_l", offs)
-        nc.sync.dma_start(out=w1_raw[1][:], in_=w1_view[:, :, H // 2 :])
+        nc.sync.dma_start(out=ds_table[:].bitcast(I32)[0:P:8, :], in_=d_scales[0].bitcast(I32))
+        nc.scalar.activation(out=warm[:, 1:2], in_=warm[:, 0:1], func=ACT.Sigmoid)
+        w1_raw = [placed("w1_raw%d" % u, [P, PACK, H // 2], F32, 8192 + 4096 * u) for u in range(2)]
+        w1_view = w1.rearrange("(p j) c -> p j c", j=PACK)
+        for u in range(2):
+            nc.sync.dma_start(out=w1_raw[u][:], in_=w1_view[:, :, u * (H // 2) : (u + 1) * (H // 2)])
         two_l = load_list("two_l", two)
         xw_table = tile("xw_table", [P, T], U32)
         nc.sync.dma_start(out=xw_table[:].bitcast(I32), in_=as_words(x_words))
         dw_table = tile("dw_table", [P, G], U32)
         nc.sync.dma_start(out=dw_table[:].bitcast(I32), in_=as_words(d_words))
-        gain = tile("gain", [P, PACK], F32)
-        nc.sync.dma_start(out=gain[:], in_=gn.rearrange("(p t) o -> p (t o)", t=PACK))
-        n1_l = load_list("n1_l", n1)
-        n2_l = load_list("n2_l", n2)
-        w2_raw = tile("w2_raw", [P, PACK, N], F32)
-        nc.sync.dma_start(out=w2_raw[:], in_=w2.rearrange("(p j) c -> p j c", j=PACK))
-        n3_l = load_list("n3_l", n3)
-        n4_l = load_list("n4_l", n4)
 
         ds_picked = tile("ds_picked", [P, H], U8)
         nc.vector.tensor_copy(out=ds_picked[:], in_=ds_table[:].indirect(k1_l[:]))
         for q in range(4):
-            nc.scalar.dma_start(
+            nc.sync.dma_start(
                 out=ds_moved[:].bitcast(I32)[32 * q : 32 * q + 4, :],
                 in_=ds_picked[:].bitcast(I32)[32 * q : 32 * q + 32 : 8, :],
             )
+        n2_l = load_list("n2_l", n2)
+        n1_l = load_list("n1_l", n1)
+        w2_raw = tile("w2_raw", [P, PACK, N], F32)
+        nc.sync.dma_start(out=w2_raw[:], in_=w2.rearrange("(p j) c -> p j c", j=PACK))
+        n3_l = load_list("n3_l", n3)
+        n4_l = load_list("n4_l", n4)
+        gain = tile("gain", [P, PACK], F32)
+        nc.gpsimd.dma_start(out=gain[:], in_=gn.rearrange("(p t) o -> p (t o)", t=PACK))
+        gain16 = tile("gain16", [P, PACK], F32)
+        nc.gpsimd.tensor_scalar(out=gain16[:], in0=gain[:], scalar1=0.0625, scalar2=0.0, op0=ALU.mult, op1=ALU.add)
         xs_offs = tile("xs_offs", [P, S], U8)
         nc.vector.tensor_copy(out=xs_offs[:], in_=xs_table[:].indirect(offs_l[:]))
         xs_two = tile("xs_two", [P, S], U8)
         nc.vector.tensor_copy(out=xs_two[:], in_=xs_table[:].indirect(two_l[:]))
 
-        w1_bf = tile("w1_bf", [P, PACK, P, PACK], BF16)
+        w1_bf = placed("w1_bf", [P, PACK, P, PACK], BF16, 0)
         for u in range(2):
             nc.scalar.copy(
                 out=w1_bf[:].rearrange("p t m j -> p m j t")[:, u * (P // 2) : (u + 1) * (P // 2)],
                 in_=w1_raw[u][:].rearrange("p j (m t) -> p m j t", t=PACK),
             )
-        xw_offs = tile("xw_offs", [P, S], U32)
-        nc.vector.tensor_copy(out=xw_offs[:], in_=xw_table[:].indirect(offs_l[:]))
         w1_codes = tile("w1_codes", [P, H], U32)
         w1_scales = tile("w1_scales", [P, H], U8)
         nc.vector.quantize_mx(
             out=w1_codes[:].bitcast(FP8X4), scales=w1_scales[:], in_=w1_bf[:].rearrange("p t m j -> p (t m j)")
         )
+        xw_offs = placed("xw_offs", [P, S], U32, 8192 + 4096)
+        nc.vector.tensor_copy(out=xw_offs[:], in_=xw_table[:].indirect(offs_l[:]))
         y_ps = [bank(t, S) for t in range(PACK)]
         for t in range(PACK):
             cols = slice(t * P, (t + 1) * P)
             mx(y_ps[t][:], w1_codes[:, cols], w1_scales[:, cols], xw_offs[:], xs_offs[:])
 
-        xw_two = tile("xw_two", [P, S], U32)
+        xw_two = placed("xw_two", [P, S], U32, 512)
         nc.vector.tensor_copy(out=xw_two[:], in_=xw_table[:].indirect(two_l[:]))
-        dw_picked = tile("dw_picked", [P, H], U32)
+        dw_picked = placed("dw_picked", [P, H], U32, 2560)
         nc.vector.tensor_copy(out=dw_picked[:], in_=dw_table[:].indirect(k1_l[:]))
-        ds_dealt = tile("ds_dealt", [P, H], U8)
+        ds_dealt = placed("ds_dealt", [P, H], U8, 0)
         nc.vector.tensor_copy(
             out=ds_dealt[:].rearrange("p (t m) -> p t m", t=PACK),
             in_=ds_moved[:].rearrange("p (m t) -> p t m", t=PACK),
@@ -135,38 +144,50 @@ def tile_picked_twkeysoftbduel_none_p_kernel(
             cols = slice(t * P, (t + 1) * P)
             mx(d_ps[t][:], dw_dealt[:, cols], ds_dealt[:, cols], xw_two[:], xs_two[:])
 
+        lc = HALF // 16
         y_rows = [tile("y_rows%d" % t, [P, S], F32) for t in range(PACK)]
         d_rows = [tile("d_rows%d" % t, [P, S], F32) for t in range(PACK)]
         d_tanh = [tile("d_tanh%d" % t, [P, S], F32) for t in range(PACK)]
-        for t in range(PACK):
-            nc.scalar.activation(out=y_rows[t][:], in_=y_ps[t][:], func=ACT.Copy, scale=gain[:, t : t + 1])
-        for t in range(PACK):
-            nc.vector.tensor_scalar(
-                out=d_rows[t][:],
-                in0=d_ps[t][:],
-                scalar1=gain[:, t : t + 1],
-                scalar2=0.0625,
-                op0=ALU.mult,
-                op1=ALU.mult,
-            )
-            nc.scalar.activation(out=d_tanh[t][:], in_=d_ps[t][:], func=ACT.Tanh, scale=0.0625)
-
-        lc = HALF // 16
         y_at = [tile("y_at%d" % u, [P, PACK, HALF], F32) for u in range(2)]
         prod = [tile("prod%d" % u, [P, PACK, HALF], F32) for u in range(2)]
-        for u in range(2):
-            for t in range(PACK):
-                nc.scalar.activation(
-                    out=y_at[u][:, t, :], in_=y_rows[t][:].indirect(n1_l[:, u * lc : (u + 1) * lc]), func=ACT.Copy
+
+        def fetch_y(t, u):
+            nc.scalar.activation(
+                out=y_at[u][:, t, :], in_=y_rows[t][:].indirect(n1_l[:, u * lc : (u + 1) * lc]), func=ACT.Copy
+            )
+
+        for t in range(PACK):
+            nc.scalar.activation(out=y_rows[t][:], in_=y_ps[t][:], func=ACT.Copy, scale=gain[:, t : t + 1])
+        for t in range(2):
+            fetch_y(t, 0)
+        for t in range(PACK):
+            if t < 2:
+                nc.vector.tensor_scalar(
+                    out=d_rows[t][:], in0=d_ps[t][:], scalar1=gain16[:, t : t + 1], scalar2=None, op0=ALU.mult
                 )
+            else:
+                nc.scalar.activation(out=d_rows[t][:], in_=d_ps[t][:], func=ACT.Copy, scale=gain16[:, t : t + 1])
+            nc.scalar.activation(out=d_tanh[t][:], in_=d_ps[t][:], func=ACT.Tanh, scale=0.0625)
+        last = PACK - 1
+        d_at = tile("d_at", [P, S], F32)
         for u in range(2):
-            for t in range(PACK):
-                nc.vector.tensor_tensor(
-                    out=prod[u][:, t, :],
-                    in0=d_rows[t][:].indirect(n2_l[:, u * lc : (u + 1) * lc]),
-                    in1=d_tanh[t][:, u * HALF : (u + 1) * HALF],
-                    op=ALU.mult,
-                )
+            nc.scalar.activation(
+                out=d_at[:, u * HALF : (u + 1) * HALF],
+                in_=d_rows[last][:].indirect(n2_l[:, u * lc : (u + 1) * lc]),
+                func=ACT.Copy,
+            )
+        for t in range(2, PACK):
+            fetch_y(t, 0)
+        for t in range(PACK):
+            fetch_y(t, 1)
+        for t in range(PACK):
+            for u in range(2):
+                cols = slice(u * HALF, (u + 1) * HALF)
+                if t == last:
+                    picked = d_at[:, cols]
+                else:
+                    picked = d_rows[t][:].indirect(n2_l[:, u * lc : (u + 1) * lc])
+                nc.vector.tensor_tensor(out=prod[u][:, t, :], in0=picked, in1=d_tanh[t][:, cols], op=ALU.mult)
 
         w2_bf = [tile("w2_bf%d" % v, [P, 2, P, PACK], BF16) for v in range(2)]
         w2_codes = [tile("w2_codes%d" % v, [P, 2 * P], U32) for v in range(2)]
@@ -212,9 +233,10 @@ def tile_picked_twkeysoftbduel_none_p_kernel(
         sig_b = [tile("sig_b%d" % t, [P, W], F32) for t in range(PACK)]
         res = [tile("res%d" % t, [P, S], F32) for t in range(PACK)]
 
+        def empty_h(t, u):
+            nc.scalar.copy(out=h_rows[t][:, u * HALF : (u + 1) * HALF], in_=h_ps[t, u][:])
+
         def fetch_pairs(t):
-            for u in range(2):
-                nc.scalar.copy(out=h_rows[t][:, u * HALF : (u + 1) * HALF], in_=h_ps[t, u][:])
             if t == 0:
                 nc.vector.tensor_copy(out=pa[t][:], in_=h_rows[t][:].indirect(n3_l[:]))
             else:
@@ -222,10 +244,18 @@ def tile_picked_twkeysoftbduel_none_p_kernel(
             nc.scalar.activation(out=pb[t][:], in_=h_rows[t][:].indirect(n4_l[:]), func=ACT.Copy)
             nc.vector.tensor_tensor(out=diff[t][:], in0=pa[t][:], in1=pb[t][:], op=ALU.subtract)
 
+        empty_h(0, 0)
+        empty_h(0, 1)
         fetch_pairs(0)
         for t in range(PACK):
             nc.scalar.activation(out=sig_a[t][:], in_=diff[t][:], func=ACT.Sigmoid)
             nc.vector.tensor_tensor(out=res[t][:].indirect(n3_l[:]), in0=pa[t][:], in1=sig_a[t][:], op=ALU.mult)
+            if t == 0:
+                empty_h(1, 0)
+            if t + 1 < PACK:
+                empty_h(t + 1, 1)
+            if t + 2 < PACK:
+                empty_h(t + 2, 0)
             if t + 1 < PACK:
                 fetch_pairs(t + 1)
             nc.scalar.activation(out=sig_b[t][:], in_=diff[t][:], func=ACT.Sigmoid, scale=-1.0)

@@ -17,7 +17,7 @@ ACT = mybir.ActivationFunctionType
 
 P = 128
 PACK = 4
-HALF = S // 2
+PIECES = (slice(0, 384), slice(384, 512))
 
 
 def tile_picked_twkeysoftbduel_none_p_kernel(
@@ -67,6 +67,8 @@ def tile_picked_twkeysoftbduel_none_p_kernel(
         nc.gpsimd.memset(ds_moved[:].bitcast(I32), 0)
 
         offs_l = load_list("offs_l", offs)
+        w1_raw = [placed("w1_raw%d" % u, [P, PACK, H // 2], F32, 8192 + 4096 * u) for u in range(2)]
+        w1_view = w1.rearrange("(p j) c -> p j c", j=PACK)
         k1_l = load_list("k1_l", k1)
         for q in range(4):
             nc.sync.dma_start(
@@ -75,8 +77,6 @@ def tile_picked_twkeysoftbduel_none_p_kernel(
             )
         nc.sync.dma_start(out=ds_table[:].bitcast(I32)[0:P:8, :], in_=d_scales[0].bitcast(I32))
         nc.scalar.activation(out=warm[:, 1:2], in_=warm[:, 0:1], func=ACT.Sigmoid)
-        w1_raw = [placed("w1_raw%d" % u, [P, PACK, H // 2], F32, 8192 + 4096 * u) for u in range(2)]
-        w1_view = w1.rearrange("(p j) c -> p j c", j=PACK)
         for u in range(2):
             nc.sync.dma_start(out=w1_raw[u][:], in_=w1_view[:, :, u * (H // 2) : (u + 1) * (H // 2)])
         two_l = load_list("two_l", two)
@@ -144,16 +144,35 @@ def tile_picked_twkeysoftbduel_none_p_kernel(
             cols = slice(t * P, (t + 1) * P)
             mx(d_ps[t][:], dw_dealt[:, cols], ds_dealt[:, cols], xw_two[:], xs_two[:])
 
-        lc = HALF // 16
-        y_rows = [tile("y_rows%d" % t, [P, S], F32) for t in range(PACK)]
+        def entries(list_tile, cols):
+            return list_tile[:, cols.start // 16 : cols.stop // 16]
+
+        wide, narrow = PIECES
+        widths = [c.stop - c.start for c in PIECES]
+        y_rows = [placed("y_rows%d" % t, [P, S], F32, 16384 + 2048 * t) for t in range(PACK)]
         d_rows = [tile("d_rows%d" % t, [P, S], F32) for t in range(PACK)]
-        d_tanh = [tile("d_tanh%d" % t, [P, S], F32) for t in range(PACK)]
-        y_at = [tile("y_at%d" % u, [P, PACK, HALF], F32) for u in range(2)]
-        prod = [tile("prod%d" % u, [P, PACK, HALF], F32) for u in range(2)]
+        d_tanh = tile("d_tanh", [P, PACK, S], F32)
+        y_at = [tile("y_at%d" % u, [P, PACK, widths[u]], F32) for u in range(2)]
+        prod = [tile("prod%d" % u, [P, PACK, widths[u]], F32) for u in range(2)]
+        d_at = tile("d_at", [P, PACK, widths[1]], F32)
 
         def fetch_y(t, u):
-            nc.scalar.activation(
-                out=y_at[u][:, t, :], in_=y_rows[t][:].indirect(n1_l[:, u * lc : (u + 1) * lc]), func=ACT.Copy
+            nc.scalar.activation(out=y_at[u][:, t, :], in_=y_rows[t][:].indirect(entries(n1_l, PIECES[u])), func=ACT.Copy)
+
+        w2_at = [16384 + 2048 * 3, 16384 + 2048 * 3 + 1024, 24576 + 1984 - 960, 48128]
+        w2_bf = [placed("w2_bf%d" % t, [P, P, PACK], BF16, w2_at[t]) for t in range(PACK)]
+        w2_codes = [tile("w2_codes%d" % t, [P, P], U32) for t in range(PACK)]
+        w2_scales = [tile("w2_scales%d" % t, [P, P], U8) for t in range(PACK)]
+
+        def round_w2(t):
+            nc.scalar.copy(
+                out=w2_bf[t][:].rearrange("p (g r) j -> p g j r", r=8),
+                in_=w2_raw[:].rearrange("p j (g t r) -> p t g j r", t=PACK, r=8)[:, t],
+            )
+
+        def quantise_w2(t):
+            nc.vector.quantize_mx(
+                out=w2_codes[t][:].bitcast(FP8X4), scales=w2_scales[t][:], in_=w2_bf[t][:].rearrange("p m j -> p (m j)")
             )
 
         for t in range(PACK):
@@ -167,74 +186,61 @@ def tile_picked_twkeysoftbduel_none_p_kernel(
                 )
             else:
                 nc.scalar.activation(out=d_rows[t][:], in_=d_ps[t][:], func=ACT.Copy, scale=gain16[:, t : t + 1])
-            nc.scalar.activation(out=d_tanh[t][:], in_=d_ps[t][:], func=ACT.Tanh, scale=0.0625)
-        last = PACK - 1
-        d_at = tile("d_at", [P, S], F32)
-        for u in range(2):
-            nc.scalar.activation(
-                out=d_at[:, u * HALF : (u + 1) * HALF],
-                in_=d_rows[last][:].indirect(n2_l[:, u * lc : (u + 1) * lc]),
-                func=ACT.Copy,
-            )
+            nc.scalar.activation(out=d_tanh[:, t, :], in_=d_ps[t][:], func=ACT.Tanh, scale=0.0625)
         for t in range(2, PACK):
             fetch_y(t, 0)
         for t in range(PACK):
-            fetch_y(t, 1)
+            nc.scalar.activation(out=d_at[:, t, :], in_=d_rows[t][:].indirect(entries(n2_l, narrow)), func=ACT.Copy)
         for t in range(PACK):
-            for u in range(2):
-                cols = slice(u * HALF, (u + 1) * HALF)
-                if t == last:
-                    picked = d_at[:, cols]
-                else:
-                    picked = d_rows[t][:].indirect(n2_l[:, u * lc : (u + 1) * lc])
-                nc.vector.tensor_tensor(out=prod[u][:, t, :], in0=picked, in1=d_tanh[t][:, cols], op=ALU.mult)
+            fetch_y(t, 1)
 
-        w2_bf = [tile("w2_bf%d" % v, [P, 2, P, PACK], BF16) for v in range(2)]
-        w2_codes = [tile("w2_codes%d" % v, [P, 2 * P], U32) for v in range(2)]
-        w2_scales = [tile("w2_scales%d" % v, [P, 2 * P], U8) for v in range(2)]
-        z_bf = [tile("z_bf%d" % u, [P, HALF, PACK], BF16) for u in range(2)]
-        z_codes = [tile("z_codes%d" % u, [P, HALF], U32) for u in range(2)]
-        z_scales = [tile("z_scales%d" % u, [P, HALF], U8) for u in range(2)]
-        for u in range(2):
-            nc.scalar.copy(
-                out=w2_bf[u][:].rearrange("p e m j -> p m j e"),
-                in_=w2_raw[:].rearrange("p j (m t) -> p m j t", t=PACK)[:, :, :, 2 * u : 2 * u + 2],
-            )
+        round_w2(0)
+        z_bf = [tile("z_bf%d" % u, [P, widths[u], PACK], BF16) for u in range(2)]
+        z_codes = tile("z_codes", [P, S], U32)
+        z_scales = tile("z_scales", [P, S], U8)
+
+        def round_z(u):
             nc.vector.tensor_tensor(
                 out=z_bf[u][:].rearrange("p (c i) t -> p c t i", i=4),
                 in0=y_at[u][:].rearrange("p t (c i) -> p c t i", i=4),
                 in1=prod[u][:].rearrange("p t (c i) -> p c t i", i=4),
                 op=ALU.subtract,
             )
+
+        def quantise_z(u):
             nc.vector.quantize_mx(
-                out=z_codes[u][:].bitcast(FP8X4), scales=z_scales[u][:], in_=z_bf[u][:].rearrange("p c t -> p (c t)")
-            )
-            nc.vector.quantize_mx(
-                out=w2_codes[u][:].bitcast(FP8X4),
-                scales=w2_scales[u][:],
-                in_=w2_bf[u][:].rearrange("p e m j -> p (e m j)"),
+                out=z_codes[:, PIECES[u]].bitcast(FP8X4),
+                scales=z_scales[:, PIECES[u]],
+                in_=z_bf[u][:].rearrange("p c t -> p (c t)"),
             )
 
-        h_ps = {}
-        for v in range(2):
-            for u in range(2):
-                for e in range(2):
-                    t = 2 * v + e
-                    h_ps[t, u] = bank(PACK * u + t, HALF)
-                    cols = slice(e * P, (e + 1) * P)
-                    mx(h_ps[t, u][:], w2_codes[v][:, cols], w2_scales[v][:, cols], z_codes[u][:], z_scales[u][:])
+        for t in range(PACK):
+            nc.vector.tensor_tensor(
+                out=prod[0][:, t, :], in0=d_rows[t][:].indirect(entries(n2_l, wide)), in1=d_tanh[:, t, wide], op=ALU.mult
+            )
+        round_z(0)
+        nc.vector.tensor_tensor(out=prod[1][:], in0=d_at[:], in1=d_tanh[:, :, narrow], op=ALU.mult)
+        quantise_z(0)
+        round_z(1)
+        quantise_w2(0)
+        quantise_z(1)
 
-        out_rows = out.rearrange("(p t) c -> t p c", t=PACK)
-        h_rows = [tile("h_rows%d" % t, [P, S], F32) for t in range(PACK)]
-        pa = [tile("pa%d" % t, [P, W], F32) for t in range(PACK)]
-        pb = [tile("pb%d" % t, [P, W], F32) for t in range(PACK)]
-        diff = [tile("diff%d" % t, [P, W], F32) for t in range(PACK)]
+        out_rows = out.rearrange("(g t r) c -> t g r c", t=PACK, r=8)
+        h_rows = [placed("h_rows%d" % t, [P, S], F32, 24576 + 1984 * t) for t in range(PACK)]
+        pa = [placed("pa%d" % t, [P, W], F32, 36864 + 2048 * t) for t in range(PACK)]
+        pb = [placed("pb%d" % t, [P, W], F32, 36864 + 2048 * t + 1024) for t in range(PACK)]
+        diff_at = [36864 + 2048 + 512, 45056, 46080, 47104]
+        diff = [placed("diff%d" % t, [P, W], F32, diff_at[t]) for t in range(PACK)]
         sig_a = [tile("sig_a%d" % t, [P, W], F32) for t in range(PACK)]
-        sig_b = [tile("sig_b%d" % t, [P, W], F32) for t in range(PACK)]
+        sig_b = [placed("sig_b%d" % t, [P, W], F32, (24576 + 1984 * (t + 1) + 64) if t < 3 else 33792) for t in range(PACK)]
         res = [tile("res%d" % t, [P, S], F32) for t in range(PACK)]
 
-        def empty_h(t, u):
-            nc.scalar.copy(out=h_rows[t][:, u * HALF : (u + 1) * HALF], in_=h_ps[t, u][:])
+        def multiply_h(t, b, passes):
+            first = passes[0].start
+            acc = bank(b, passes[-1].stop - first)
+            for c in passes:
+                mx(acc[:, c.start - first : c.stop - first], w2_codes[t][:], w2_scales[t][:], z_codes[:, c], z_scales[:, c])
+            nc.scalar.copy(out=h_rows[t][:, first : passes[-1].stop], in_=acc[:])
 
         def fetch_pairs(t):
             if t == 0:
@@ -244,20 +250,26 @@ def tile_picked_twkeysoftbduel_none_p_kernel(
             nc.scalar.activation(out=pb[t][:], in_=h_rows[t][:].indirect(n4_l[:]), func=ACT.Copy)
             nc.vector.tensor_tensor(out=diff[t][:], in0=pa[t][:], in1=pb[t][:], op=ALU.subtract)
 
-        empty_h(0, 0)
-        empty_h(0, 1)
+        multiply_h(0, 0, [slice(0, 256), slice(256, 384)])
+        round_w2(1)
+        multiply_h(0, 1, [narrow])
+        quantise_w2(1)
         fetch_pairs(0)
+        back0 = placed("back0", [P, W], F32, 48128)
+        nc.vector.tensor_tensor(out=back0[:], in0=pb[0][:], in1=pa[0][:], op=ALU.subtract)
         for t in range(PACK):
             nc.scalar.activation(out=sig_a[t][:], in_=diff[t][:], func=ACT.Sigmoid)
             nc.vector.tensor_tensor(out=res[t][:].indirect(n3_l[:]), in0=pa[t][:], in1=sig_a[t][:], op=ALU.mult)
-            if t == 0:
-                empty_h(1, 0)
             if t + 1 < PACK:
-                empty_h(t + 1, 1)
-            if t + 2 < PACK:
-                empty_h(t + 2, 0)
-            if t + 1 < PACK:
+                multiply_h(t + 1, 2 + t, [slice(0, S)])
                 fetch_pairs(t + 1)
-            nc.scalar.activation(out=sig_b[t][:], in_=diff[t][:], func=ACT.Sigmoid, scale=-1.0)
+            if t == 0:
+                round_w2(2)
+                quantise_w2(2)
+                nc.scalar.activation(out=sig_b[t][:], in_=back0[:], func=ACT.Sigmoid)
+                round_w2(3)
+                quantise_w2(3)
+            else:
+                nc.scalar.activation(out=sig_b[t][:], in_=diff[t][:], func=ACT.Sigmoid, scale=-1.0)
             nc.vector.tensor_tensor(out=res[t][:].indirect(n4_l[:]), in0=pb[t][:], in1=sig_b[t][:], op=ALU.mult)
             nc.sync.dma_start(out=out_rows[t], in_=res[t][:])

@@ -3,7 +3,7 @@ from contextlib import ExitStack
 import concourse.mybir as mybir
 
 K, T, S, N, H, G, W = 512, 2048, 512, 512, 512, 2048, 256
-FLOPS = 2 * K * H * S * 2 + 2 * H * N * S
+FLOPS = 2 * (2 * K * H * S) + 2 * H * N * S
 
 F32 = mybir.dt.float32
 BF16 = mybir.dt.bfloat16
@@ -17,7 +17,25 @@ ACT = mybir.ActivationFunctionType
 
 P = 128
 PACK = 4
-PIECES = (slice(0, 384), slice(384, 512))
+QUADRANTS = 4
+SIXTEENTH = 0.0625
+HALVES = (slice(0, S // 2), slice(S // 2, S))
+HALF = S // 2
+D_PLANES_ON_VECTOR = 2
+Y_PLANES_AHEAD = 2
+
+LINE = 64
+ROW = 4 * S
+PAIR = 4 * W
+W1_BF_AT = 0
+DS_DEALT_AT = W1_BF_AT
+XW_TWO_AT = DS_DEALT_AT + H
+DW_PICKED_AT = XW_TWO_AT + ROW
+W1_RAW_AT = DW_PICKED_AT + ROW
+XW_OFFS_AT = W1_RAW_AT + 2 * ROW
+H_AT = W1_RAW_AT + 4 * ROW
+H_STEP = ROW - LINE
+PAIRS_AT = H_AT + PACK * ROW
 
 
 def tile_picked_twkeysoftbduel_none_p_kernel(
@@ -26,27 +44,33 @@ def tile_picked_twkeysoftbduel_none_p_kernel(
     nc = tc.nc
     with ExitStack() as ctx:
         sb = ctx.enter_context(tc.tile_pool(name="sb", bufs=1))
-        shared = ctx.enter_context(tc.tile_pool(name="shared", bufs=1))
+        reused = ctx.enter_context(tc.tile_pool(name="reused", bufs=1))
         ps = ctx.enter_context(tc.psum_pool(name="ps", bufs=1))
 
         def tile(name, shape, dtype):
-            return sb.tile(shape, dtype, name=name, align_bytes=64)
+            return sb.tile(shape, dtype, name=name, align_bytes=LINE)
 
         def placed(name, shape, dtype, offset):
-            return shared.tile(shape, dtype, name=name, align_bytes=64, offset=offset)
+            return reused.tile(shape, dtype, name=name, align_bytes=LINE, offset=offset)
 
         def bank(b, width):
             return ps.tile([P, width], F32, name="bank%d" % b)
 
         def load_list(name, src):
-            t = sb.tile(list(src.shape), U16, name=name)
-            nc.sync.dma_start(t[:], src)
-            return t
+            list_tile = sb.tile(list(src.shape), U16, name=name)
+            nc.sync.dma_start(list_tile[:], src)
+            return list_tile
+
+        def entries(list_tile, cols):
+            return list_tile[:, cols.start // 16 : cols.stop // 16]
 
         def as_words(dram):
             return dram[0].rearrange("p n r -> p (n r)").bitcast(I32)
 
-        def mx(acc, lhs_codes, lhs_scales, rhs_codes, rhs_scales):
+        def quantise(codes, scales, rounded):
+            nc.vector.quantize_mx(out=codes.bitcast(FP8X4), scales=scales, in_=rounded)
+
+        def multiply(acc, lhs_codes, lhs_scales, rhs_codes, rhs_scales):
             nc.tensor.matmul_mx(
                 out=acc,
                 lhsT=lhs_codes.bitcast(FP8X4),
@@ -67,16 +91,16 @@ def tile_picked_twkeysoftbduel_none_p_kernel(
         nc.gpsimd.memset(ds_moved[:].bitcast(I32), 0)
 
         offs_l = load_list("offs_l", offs)
-        w1_raw = [placed("w1_raw%d" % u, [P, PACK, H // 2], F32, 8192 + 4096 * u) for u in range(2)]
-        w1_view = w1.rearrange("(p j) c -> p j c", j=PACK)
         k1_l = load_list("k1_l", k1)
-        for q in range(4):
+        for q in range(QUADRANTS):
             nc.sync.dma_start(
                 out=xs_table[:].bitcast(I32)[32 * q : 32 * q + 4, :],
                 in_=x_scales[0].bitcast(I32)[4 * q : 4 * q + 4, :],
             )
         nc.sync.dma_start(out=ds_table[:].bitcast(I32)[0:P:8, :], in_=d_scales[0].bitcast(I32))
         nc.scalar.activation(out=warm[:, 1:2], in_=warm[:, 0:1], func=ACT.Sigmoid)
+        w1_raw = [placed("w1_raw%d" % u, [P, PACK, H // 2], F32, W1_RAW_AT + 2 * ROW * u) for u in range(2)]
+        w1_view = w1.rearrange("(p j) c -> p j c", j=PACK)
         for u in range(2):
             nc.sync.dma_start(out=w1_raw[u][:], in_=w1_view[:, :, u * (H // 2) : (u + 1) * (H // 2)])
         two_l = load_list("two_l", two)
@@ -87,7 +111,7 @@ def tile_picked_twkeysoftbduel_none_p_kernel(
 
         ds_picked = tile("ds_picked", [P, H], U8)
         nc.vector.tensor_copy(out=ds_picked[:], in_=ds_table[:].indirect(k1_l[:]))
-        for q in range(4):
+        for q in range(QUADRANTS):
             nc.sync.dma_start(
                 out=ds_moved[:].bitcast(I32)[32 * q : 32 * q + 4, :],
                 in_=ds_picked[:].bitcast(I32)[32 * q : 32 * q + 32 : 8, :],
@@ -101,13 +125,14 @@ def tile_picked_twkeysoftbduel_none_p_kernel(
         gain = tile("gain", [P, PACK], F32)
         nc.gpsimd.dma_start(out=gain[:], in_=gn.rearrange("(p t) o -> p (t o)", t=PACK))
         gain16 = tile("gain16", [P, PACK], F32)
-        nc.gpsimd.tensor_scalar(out=gain16[:], in0=gain[:], scalar1=0.0625, scalar2=0.0, op0=ALU.mult, op1=ALU.add)
+        nc.gpsimd.tensor_scalar(out=gain16[:], in0=gain[:], scalar1=SIXTEENTH, scalar2=0.0, op0=ALU.mult, op1=ALU.add)
+
         xs_offs = tile("xs_offs", [P, S], U8)
         nc.vector.tensor_copy(out=xs_offs[:], in_=xs_table[:].indirect(offs_l[:]))
         xs_two = tile("xs_two", [P, S], U8)
         nc.vector.tensor_copy(out=xs_two[:], in_=xs_table[:].indirect(two_l[:]))
 
-        w1_bf = placed("w1_bf", [P, PACK, P, PACK], BF16, 0)
+        w1_bf = placed("w1_bf", [P, PACK, P, PACK], BF16, W1_BF_AT)
         for u in range(2):
             nc.scalar.copy(
                 out=w1_bf[:].rearrange("p t m j -> p m j t")[:, u * (P // 2) : (u + 1) * (P // 2)],
@@ -115,21 +140,19 @@ def tile_picked_twkeysoftbduel_none_p_kernel(
             )
         w1_codes = tile("w1_codes", [P, H], U32)
         w1_scales = tile("w1_scales", [P, H], U8)
-        nc.vector.quantize_mx(
-            out=w1_codes[:].bitcast(FP8X4), scales=w1_scales[:], in_=w1_bf[:].rearrange("p t m j -> p (t m j)")
-        )
-        xw_offs = placed("xw_offs", [P, S], U32, 8192 + 4096)
+        quantise(w1_codes[:], w1_scales[:], w1_bf[:].rearrange("p t m j -> p (t m j)"))
+        xw_offs = placed("xw_offs", [P, S], U32, XW_OFFS_AT)
         nc.vector.tensor_copy(out=xw_offs[:], in_=xw_table[:].indirect(offs_l[:]))
         y_ps = [bank(t, S) for t in range(PACK)]
         for t in range(PACK):
             cols = slice(t * P, (t + 1) * P)
-            mx(y_ps[t][:], w1_codes[:, cols], w1_scales[:, cols], xw_offs[:], xs_offs[:])
+            multiply(y_ps[t][:], w1_codes[:, cols], w1_scales[:, cols], xw_offs[:], xs_offs[:])
 
-        xw_two = placed("xw_two", [P, S], U32, 512)
+        xw_two = placed("xw_two", [P, S], U32, XW_TWO_AT)
         nc.vector.tensor_copy(out=xw_two[:], in_=xw_table[:].indirect(two_l[:]))
-        dw_picked = placed("dw_picked", [P, H], U32, 2560)
+        dw_picked = placed("dw_picked", [P, H], U32, DW_PICKED_AT)
         nc.vector.tensor_copy(out=dw_picked[:], in_=dw_table[:].indirect(k1_l[:]))
-        ds_dealt = placed("ds_dealt", [P, H], U8, 0)
+        ds_dealt = placed("ds_dealt", [P, H], U8, DS_DEALT_AT)
         nc.vector.tensor_copy(
             out=ds_dealt[:].rearrange("p (t m) -> p t m", t=PACK),
             in_=ds_moved[:].rearrange("p (m t) -> p t m", t=PACK),
@@ -142,105 +165,92 @@ def tile_picked_twkeysoftbduel_none_p_kernel(
         d_ps = [bank(PACK + t, S) for t in range(PACK)]
         for t in range(PACK):
             cols = slice(t * P, (t + 1) * P)
-            mx(d_ps[t][:], dw_dealt[:, cols], ds_dealt[:, cols], xw_two[:], xs_two[:])
+            multiply(d_ps[t][:], dw_dealt[:, cols], ds_dealt[:, cols], xw_two[:], xs_two[:])
 
-        def entries(list_tile, cols):
-            return list_tile[:, cols.start // 16 : cols.stop // 16]
-
-        wide, narrow = PIECES
-        widths = [c.stop - c.start for c in PIECES]
-        y_rows = [placed("y_rows%d" % t, [P, S], F32, 16384 + 2048 * t) for t in range(PACK)]
+        y_rows = [tile("y_rows%d" % t, [P, S], F32) for t in range(PACK)]
         d_rows = [tile("d_rows%d" % t, [P, S], F32) for t in range(PACK)]
         d_tanh = tile("d_tanh", [P, PACK, S], F32)
-        y_at = [tile("y_at%d" % u, [P, PACK, widths[u]], F32) for u in range(2)]
-        prod = [tile("prod%d" % u, [P, PACK, widths[u]], F32) for u in range(2)]
-        d_at = tile("d_at", [P, PACK, widths[1]], F32)
+        y_at = [tile("y_at%d" % u, [P, PACK, HALF], F32) for u in range(2)]
+        prod = [tile("prod%d" % u, [P, PACK, HALF], F32) for u in range(2)]
 
         def fetch_y(t, u):
-            nc.scalar.activation(out=y_at[u][:, t, :], in_=y_rows[t][:].indirect(entries(n1_l, PIECES[u])), func=ACT.Copy)
-
-        w2_at = [16384 + 2048 * 3, 16384 + 2048 * 3 + 1024, 24576 + 1984 - 960, 48128]
-        w2_bf = [placed("w2_bf%d" % t, [P, P, PACK], BF16, w2_at[t]) for t in range(PACK)]
-        w2_codes = [tile("w2_codes%d" % t, [P, P], U32) for t in range(PACK)]
-        w2_scales = [tile("w2_scales%d" % t, [P, P], U8) for t in range(PACK)]
-
-        def round_w2(t):
-            nc.scalar.copy(
-                out=w2_bf[t][:].rearrange("p (g r) j -> p g j r", r=8),
-                in_=w2_raw[:].rearrange("p j (g t r) -> p t g j r", t=PACK, r=8)[:, t],
-            )
-
-        def quantise_w2(t):
-            nc.vector.quantize_mx(
-                out=w2_codes[t][:].bitcast(FP8X4), scales=w2_scales[t][:], in_=w2_bf[t][:].rearrange("p m j -> p (m j)")
+            nc.scalar.activation(
+                out=y_at[u][:, t, :], in_=y_rows[t][:].indirect(entries(n1_l, HALVES[u])), func=ACT.Copy
             )
 
         for t in range(PACK):
             nc.scalar.activation(out=y_rows[t][:], in_=y_ps[t][:], func=ACT.Copy, scale=gain[:, t : t + 1])
-        for t in range(2):
+        for t in range(Y_PLANES_AHEAD):
             fetch_y(t, 0)
         for t in range(PACK):
-            if t < 2:
+            if t < D_PLANES_ON_VECTOR:
                 nc.vector.tensor_scalar(
                     out=d_rows[t][:], in0=d_ps[t][:], scalar1=gain16[:, t : t + 1], scalar2=None, op0=ALU.mult
                 )
             else:
                 nc.scalar.activation(out=d_rows[t][:], in_=d_ps[t][:], func=ACT.Copy, scale=gain16[:, t : t + 1])
-            nc.scalar.activation(out=d_tanh[:, t, :], in_=d_ps[t][:], func=ACT.Tanh, scale=0.0625)
-        for t in range(2, PACK):
+            nc.scalar.activation(out=d_tanh[:, t, :], in_=d_ps[t][:], func=ACT.Tanh, scale=SIXTEENTH)
+        for t in range(Y_PLANES_AHEAD, PACK):
             fetch_y(t, 0)
-        for t in range(PACK):
-            nc.scalar.activation(out=d_at[:, t, :], in_=d_rows[t][:].indirect(entries(n2_l, narrow)), func=ACT.Copy)
         for t in range(PACK):
             fetch_y(t, 1)
 
-        round_w2(0)
-        z_bf = [tile("z_bf%d" % u, [P, widths[u], PACK], BF16) for u in range(2)]
+        w2_bf = [tile("w2_bf%d" % v, [P, 2, P, PACK], BF16) for v in range(2)]
+        w2_codes = [tile("w2_codes%d" % v, [P, 2 * P], U32) for v in range(2)]
+        w2_scales = [tile("w2_scales%d" % v, [P, 2 * P], U8) for v in range(2)]
+
+        def round_w2(v):
+            nc.scalar.copy(
+                out=w2_bf[v][:].rearrange("p e m j -> p m j e"),
+                in_=w2_raw[:].rearrange("p j (m t) -> p m j t", t=PACK)[:, :, :, 2 * v : 2 * v + 2],
+            )
+
+        def quantise_w2(v):
+            quantise(w2_codes[v][:], w2_scales[v][:], w2_bf[v][:].rearrange("p e m j -> p (e m j)"))
+
+        z_bf = [tile("z_bf%d" % u, [P, HALF, PACK], BF16) for u in range(2)]
         z_codes = tile("z_codes", [P, S], U32)
         z_scales = tile("z_scales", [P, S], U8)
 
-        def round_z(u):
+        def quantise_z(u):
             nc.vector.tensor_tensor(
                 out=z_bf[u][:].rearrange("p (c i) t -> p c t i", i=4),
                 in0=y_at[u][:].rearrange("p t (c i) -> p c t i", i=4),
                 in1=prod[u][:].rearrange("p t (c i) -> p c t i", i=4),
                 op=ALU.subtract,
             )
+            quantise(z_codes[:, HALVES[u]], z_scales[:, HALVES[u]], z_bf[u][:].rearrange("p c t -> p (c t)"))
 
-        def quantise_z(u):
-            nc.vector.quantize_mx(
-                out=z_codes[:, PIECES[u]].bitcast(FP8X4),
-                scales=z_scales[:, PIECES[u]],
-                in_=z_bf[u][:].rearrange("p c t -> p (c t)"),
-            )
-
+        round_w2(0)
         for t in range(PACK):
-            nc.vector.tensor_tensor(
-                out=prod[0][:, t, :], in0=d_rows[t][:].indirect(entries(n2_l, wide)), in1=d_tanh[:, t, wide], op=ALU.mult
-            )
-        round_z(0)
-        nc.vector.tensor_tensor(out=prod[1][:], in0=d_at[:], in1=d_tanh[:, :, narrow], op=ALU.mult)
+            for u in range(2):
+                nc.vector.tensor_tensor(
+                    out=prod[u][:, t, :],
+                    in0=d_rows[t][:].indirect(entries(n2_l, HALVES[u])),
+                    in1=d_tanh[:, t, HALVES[u]],
+                    op=ALU.mult,
+                )
         quantise_z(0)
-        round_z(1)
         quantise_w2(0)
         quantise_z(1)
 
-        out_rows = out.rearrange("(g t r) c -> t g r c", t=PACK, r=8)
-        h_rows = [placed("h_rows%d" % t, [P, S], F32, 24576 + 1984 * t) for t in range(PACK)]
-        pa = [placed("pa%d" % t, [P, W], F32, 36864 + 2048 * t) for t in range(PACK)]
-        pb = [placed("pb%d" % t, [P, W], F32, 36864 + 2048 * t + 1024) for t in range(PACK)]
-        diff_at = [36864 + 2048 + 512, 45056, 46080, 47104]
-        diff = [placed("diff%d" % t, [P, W], F32, diff_at[t]) for t in range(PACK)]
+        last = PACK - 1
+        out_rows = out.rearrange("(p t) c -> t p c", t=PACK)
+        h_rows = [placed("h_rows%d" % t, [P, S], F32, H_AT + H_STEP * t) for t in range(PACK)]
+        pa = [placed("pa%d" % t, [P, W], F32, PAIRS_AT + 2 * PAIR * t) for t in range(PACK)]
+        pb = [placed("pb%d" % t, [P, W], F32, PAIRS_AT + 2 * PAIR * t + PAIR) for t in range(PACK)]
+        a_less_b = [placed("a_less_b0", [P, W], F32, PAIRS_AT + 2 * PAIR + PAIR // 2)]
+        a_less_b.extend(tile("a_less_b%d" % t, [P, W], F32) for t in range(1, PACK))
         sig_a = [tile("sig_a%d" % t, [P, W], F32) for t in range(PACK)]
-        sig_b = [placed("sig_b%d" % t, [P, W], F32, (24576 + 1984 * (t + 1) + 64) if t < 3 else 33792) for t in range(PACK)]
+        sig_b = [placed("sig_b%d" % t, [P, W], F32, H_AT + H_STEP * (t + 1) + LINE) for t in range(last)]
+        sig_b.append(tile("sig_b%d" % last, [P, W], F32))
         res = [tile("res%d" % t, [P, S], F32) for t in range(PACK)]
 
-        def multiply_h(t, b, passes):
-            first = passes[0].start
-            acc = bank(b, passes[-1].stop - first)
-            for c in passes:
-                mx(acc[:, c.start - first : c.stop - first], w2_codes[t][:], w2_scales[t][:], z_codes[:, c], z_scales[:, c])
-            nc.scalar.copy(out=h_rows[t][:, first : passes[-1].stop], in_=acc[:])
+        def multiply_h(t, b, cols):
+            acc = bank(b, cols.stop - cols.start)
+            plane = slice(t % 2 * P, (t % 2 + 1) * P)
+            multiply(acc[:], w2_codes[t // 2][:, plane], w2_scales[t // 2][:, plane], z_codes[:, cols], z_scales[:, cols])
+            nc.scalar.copy(out=h_rows[t][:, cols], in_=acc[:])
 
         def fetch_pairs(t):
             if t == 0:
@@ -248,28 +258,24 @@ def tile_picked_twkeysoftbduel_none_p_kernel(
             else:
                 nc.scalar.activation(out=pa[t][:], in_=h_rows[t][:].indirect(n3_l[:]), func=ACT.Copy)
             nc.scalar.activation(out=pb[t][:], in_=h_rows[t][:].indirect(n4_l[:]), func=ACT.Copy)
-            nc.vector.tensor_tensor(out=diff[t][:], in0=pa[t][:], in1=pb[t][:], op=ALU.subtract)
+            nc.vector.tensor_tensor(out=a_less_b[t][:], in0=pa[t][:], in1=pb[t][:], op=ALU.subtract)
 
-        multiply_h(0, 0, [slice(0, 256), slice(256, 384)])
+        multiply_h(0, 0, HALVES[0])
         round_w2(1)
-        multiply_h(0, 1, [narrow])
+        multiply_h(0, 1, HALVES[1])
         quantise_w2(1)
         fetch_pairs(0)
-        back0 = placed("back0", [P, W], F32, 48128)
-        nc.vector.tensor_tensor(out=back0[:], in0=pb[0][:], in1=pa[0][:], op=ALU.subtract)
+        b_less_a0 = tile("b_less_a0", [P, W], F32)
+        nc.vector.tensor_tensor(out=b_less_a0[:], in0=pb[0][:], in1=pa[0][:], op=ALU.subtract)
         for t in range(PACK):
-            nc.scalar.activation(out=sig_a[t][:], in_=diff[t][:], func=ACT.Sigmoid)
+            nc.scalar.activation(out=sig_a[t][:], in_=a_less_b[t][:], func=ACT.Sigmoid)
             nc.vector.tensor_tensor(out=res[t][:].indirect(n3_l[:]), in0=pa[t][:], in1=sig_a[t][:], op=ALU.mult)
-            if t + 1 < PACK:
-                multiply_h(t + 1, 2 + t, [slice(0, S)])
+            if t < last:
+                multiply_h(t + 1, 2 + t, slice(0, S))
                 fetch_pairs(t + 1)
             if t == 0:
-                round_w2(2)
-                quantise_w2(2)
-                nc.scalar.activation(out=sig_b[t][:], in_=back0[:], func=ACT.Sigmoid)
-                round_w2(3)
-                quantise_w2(3)
+                nc.scalar.activation(out=sig_b[t][:], in_=b_less_a0[:], func=ACT.Sigmoid)
             else:
-                nc.scalar.activation(out=sig_b[t][:], in_=diff[t][:], func=ACT.Sigmoid, scale=-1.0)
+                nc.scalar.activation(out=sig_b[t][:], in_=a_less_b[t][:], func=ACT.Sigmoid, scale=-1.0)
             nc.vector.tensor_tensor(out=res[t][:].indirect(n4_l[:]), in0=pb[t][:], in1=sig_b[t][:], op=ALU.mult)
             nc.sync.dma_start(out=out_rows[t], in_=res[t][:])

from contextlib import ExitStack

import concourse.mybir as mybir

K, T, S, N, H, G, W = 512, 2048, 512, 512, 512, 2048, 256
FLOPS = 2 * (2 * K * H * S) + 2 * H * N * S

F32 = mybir.dt.float32
BF16 = mybir.dt.bfloat16
I32 = mybir.dt.int32
U32 = mybir.dt.uint32
U16 = mybir.dt.uint16
U8 = mybir.dt.uint8
FP8X4 = mybir.dt.float8_e4m3fn_x4
ALU = mybir.AluOpType
ACT = mybir.ActivationFunctionType

P = 128
PACK = 4
QUADRANTS = 4
SIXTEENTH = 0.0625
HALVES = (slice(0, S // 2), slice(S // 2, S))
HALF = S // 2
D_PLANES_ON_VECTOR = 2
Y_PLANES_AHEAD = 2

LINE = 64
ROW = 4 * S
PAIR = 4 * W
W1_BF_AT = 0
DS_DEALT_AT = W1_BF_AT
XW_TWO_AT = DS_DEALT_AT + H
DW_PICKED_AT = XW_TWO_AT + ROW
W1_RAW_AT = DW_PICKED_AT + ROW
XW_OFFS_AT = W1_RAW_AT + 2 * ROW
H_AT = W1_RAW_AT + 4 * ROW
H_STEP = ROW - LINE
PAIRS_AT = H_AT + PACK * ROW


def tile_picked_twkeysoftbduel_none_p_kernel(
    tc, x_words, x_scales, w1, d_words, d_scales, gn, w2, offs, k1, two, n1, n2, n3, n4, out
):
    nc = tc.nc
    with ExitStack() as ctx:
        sb = ctx.enter_context(tc.tile_pool(name="sb", bufs=1))
        reused = ctx.enter_context(tc.tile_pool(name="reused", bufs=1))
        ps = ctx.enter_context(tc.psum_pool(name="ps", bufs=1))

        def tile(name, shape, dtype):
            return sb.tile(shape, dtype, name=name, align_bytes=LINE)

        def placed(name, shape, dtype, offset):
            return reused.tile(shape, dtype, name=name, align_bytes=LINE, offset=offset)

        def bank(b, width):
            return ps.tile([P, width], F32, name="bank%d" % b)

        def load_list(name, src):
            list_tile = sb.tile(list(src.shape), U16, name=name)
            nc.sync.dma_start(list_tile[:], src)
            return list_tile

        def entries(list_tile, cols):
            return list_tile[:, cols.start // 16 : cols.stop // 16]

        def as_words(dram):
            return dram[0].rearrange("p n r -> p (n r)").bitcast(I32)

        def quantise(codes, scales, rounded):
            nc.vector.quantize_mx(out=codes.bitcast(FP8X4), scales=scales, in_=rounded)

        def multiply(acc, lhs_codes, lhs_scales, rhs_codes, rhs_scales):
            nc.tensor.matmul_mx(
                out=acc,
                lhsT=lhs_codes.bitcast(FP8X4),
                lhsT_scale=lhs_scales,
                rhs=rhs_codes.bitcast(FP8X4),
                rhs_scale=rhs_scales,
                start=True,
                stop=True,
            )

        xs_table = tile("xs_table", [P, T], U8)
        ds_table = tile("ds_table", [P, G], U8)
        ds_moved = tile("ds_moved", [P, H], U8)
        nc.gpsimd.memset(xs_table[:].bitcast(I32), 0)
        nc.vector.memset(ds_table[:].bitcast(I32), 0)
        warm = tile("warm", [P, 2], F32)
        nc.vector.memset(warm[:, 0:1], 0.0)
        nc.gpsimd.memset(ds_moved[:].bitcast(I32), 0)

        offs_l = load_list("offs_l", offs)
        k1_l = load_list("k1_l", k1)
        for q in range(QUADRANTS):
            nc.sync.dma_start(
                out=xs_table[:].bitcast(I32)[32 * q : 32 * q + 4, :],
                in_=x_scales[0].bitcast(I32)[4 * q : 4 * q + 4, :],
            )
        nc.sync.dma_start(out=ds_table[:].bitcast(I32)[0:P:8, :], in_=d_scales[0].bitcast(I32))
        nc.scalar.activation(out=warm[:, 1:2], in_=warm[:, 0:1], func=ACT.Sigmoid)
        w1_raw = [placed("w1_raw%d" % u, [P, PACK, H // 2], F32, W1_RAW_AT + 2 * ROW * u) for u in range(2)]
        w1_view = w1.rearrange("(p j) c -> p j c", j=PACK)
        for u in range(2):
            nc.sync.dma_start(out=w1_raw[u][:], in_=w1_view[:, :, u * (H // 2) : (u + 1) * (H // 2)])
        two_l = load_list("two_l", two)
        xw_table = tile("xw_table", [P, T], U32)
        nc.sync.dma_start(out=xw_table[:].bitcast(I32), in_=as_words(x_words))
        dw_table = tile("dw_table", [P, G], U32)
        nc.sync.dma_start(out=dw_table[:].bitcast(I32), in_=as_words(d_words))

        ds_picked = tile("ds_picked", [P, H], U8)
        nc.vector.tensor_copy(out=ds_picked[:], in_=ds_table[:].indirect(k1_l[:]))
        for q in range(QUADRANTS):
            nc.sync.dma_start(
                out=ds_moved[:].bitcast(I32)[32 * q : 32 * q + 4, :],
                in_=ds_picked[:].bitcast(I32)[32 * q : 32 * q + 32 : 8, :],
            )
        n2_l = load_list("n2_l", n2)
        n1_l = load_list("n1_l", n1)
        w2_raw = tile("w2_raw", [P, PACK, N], F32)
        nc.sync.dma_start(out=w2_raw[:], in_=w2.rearrange("(p j) c -> p j c", j=PACK))
        n3_l = load_list("n3_l", n3)
        n4_l = load_list("n4_l", n4)
        gain = tile("gain", [P, PACK], F32)
        nc.gpsimd.dma_start(out=gain[:], in_=gn.rearrange("(p t) o -> p (t o)", t=PACK))
        gain16 = tile("gain16", [P, PACK], F32)
        nc.gpsimd.tensor_scalar(out=gain16[:], in0=gain[:], scalar1=SIXTEENTH, scalar2=0.0, op0=ALU.mult, op1=ALU.add)

        xs_offs = tile("xs_offs", [P, S], U8)
        nc.vector.tensor_copy(out=xs_offs[:], in_=xs_table[:].indirect(offs_l[:]))
        xs_two = tile("xs_two", [P, S], U8)
        nc.vector.tensor_copy(out=xs_two[:], in_=xs_table[:].indirect(two_l[:]))

        w1_bf = placed("w1_bf", [P, PACK, P, PACK], BF16, W1_BF_AT)
        for u in range(2):
            nc.scalar.copy(
                out=w1_bf[:].rearrange("p t m j -> p m j t")[:, u * (P // 2) : (u + 1) * (P // 2)],
                in_=w1_raw[u][:].rearrange("p j (m t) -> p m j t", t=PACK),
            )
        w1_codes = tile("w1_codes", [P, H], U32)
        w1_scales = tile("w1_scales", [P, H], U8)
        quantise(w1_codes[:], w1_scales[:], w1_bf[:].rearrange("p t m j -> p (t m j)"))
        xw_offs = placed("xw_offs", [P, S], U32, XW_OFFS_AT)
        nc.vector.tensor_copy(out=xw_offs[:], in_=xw_table[:].indirect(offs_l[:]))
        y_ps = [bank(t, S) for t in range(PACK)]
        for t in range(PACK):
            cols = slice(t * P, (t + 1) * P)
            multiply(y_ps[t][:], w1_codes[:, cols], w1_scales[:, cols], xw_offs[:], xs_offs[:])

        xw_two = placed("xw_two", [P, S], U32, XW_TWO_AT)
        nc.vector.tensor_copy(out=xw_two[:], in_=xw_table[:].indirect(two_l[:]))
        dw_picked = placed("dw_picked", [P, H], U32, DW_PICKED_AT)
        nc.vector.tensor_copy(out=dw_picked[:], in_=dw_table[:].indirect(k1_l[:]))
        ds_dealt = placed("ds_dealt", [P, H], U8, DS_DEALT_AT)
        nc.vector.tensor_copy(
            out=ds_dealt[:].rearrange("p (t m) -> p t m", t=PACK),
            in_=ds_moved[:].rearrange("p (m t) -> p t m", t=PACK),
        )
        dw_dealt = tile("dw_dealt", [P, H], U32)
        nc.vector.tensor_copy(
            out=dw_dealt[:].rearrange("p (t m) -> p m t", t=PACK),
            in_=dw_picked[:].rearrange("p (m t) -> p m t", t=PACK),
        )
        d_ps = [bank(PACK + t, S) for t in range(PACK)]
        for t in range(PACK):
            cols = slice(t * P, (t + 1) * P)
            multiply(d_ps[t][:], dw_dealt[:, cols], ds_dealt[:, cols], xw_two[:], xs_two[:])

        y_rows = [tile("y_rows%d" % t, [P, S], F32) for t in range(PACK)]
        d_rows = [tile("d_rows%d" % t, [P, S], F32) for t in range(PACK)]
        d_tanh = tile("d_tanh", [P, PACK, S], F32)
        y_at = [tile("y_at%d" % u, [P, PACK, HALF], F32) for u in range(2)]
        prod = [tile("prod%d" % u, [P, PACK, HALF], F32) for u in range(2)]

        def fetch_y(t, u):
            nc.scalar.activation(
                out=y_at[u][:, t, :], in_=y_rows[t][:].indirect(entries(n1_l, HALVES[u])), func=ACT.Copy
            )

        for t in range(PACK):
            nc.scalar.activation(out=y_rows[t][:], in_=y_ps[t][:], func=ACT.Copy, scale=gain[:, t : t + 1])
        for t in range(Y_PLANES_AHEAD):
            fetch_y(t, 0)
        for t in range(PACK):
            if t < D_PLANES_ON_VECTOR:
                nc.vector.tensor_scalar(
                    out=d_rows[t][:], in0=d_ps[t][:], scalar1=gain16[:, t : t + 1], scalar2=None, op0=ALU.mult
                )
            else:
                nc.scalar.activation(out=d_rows[t][:], in_=d_ps[t][:], func=ACT.Copy, scale=gain16[:, t : t + 1])
            nc.scalar.activation(out=d_tanh[:, t, :], in_=d_ps[t][:], func=ACT.Tanh, scale=SIXTEENTH)
        for t in range(Y_PLANES_AHEAD, PACK):
            fetch_y(t, 0)
        for t in range(PACK):
            fetch_y(t, 1)

        w2_bf = [tile("w2_bf%d" % v, [P, 2, P, PACK], BF16) for v in range(2)]
        w2_codes = [tile("w2_codes%d" % v, [P, 2 * P], U32) for v in range(2)]
        w2_scales = [tile("w2_scales%d" % v, [P, 2 * P], U8) for v in range(2)]

        def round_w2(v):
            nc.scalar.copy(
                out=w2_bf[v][:].rearrange("p e m j -> p m j e"),
                in_=w2_raw[:].rearrange("p j (m t) -> p m j t", t=PACK)[:, :, :, 2 * v : 2 * v + 2],
            )

        def quantise_w2(v):
            quantise(w2_codes[v][:], w2_scales[v][:], w2_bf[v][:].rearrange("p e m j -> p (e m j)"))

        z_bf = [tile("z_bf%d" % u, [P, HALF, PACK], BF16) for u in range(2)]
        z_codes = tile("z_codes", [P, S], U32)
        z_scales = tile("z_scales", [P, S], U8)

        def quantise_z(u):
            nc.vector.tensor_tensor(
                out=z_bf[u][:].rearrange("p (c i) t -> p c t i", i=4),
                in0=y_at[u][:].rearrange("p t (c i) -> p c t i", i=4),
                in1=prod[u][:].rearrange("p t (c i) -> p c t i", i=4),
                op=ALU.subtract,
            )
            quantise(z_codes[:, HALVES[u]], z_scales[:, HALVES[u]], z_bf[u][:].rearrange("p c t -> p (c t)"))

        round_w2(0)
        for t in range(PACK):
            for u in range(2):
                nc.vector.tensor_tensor(
                    out=prod[u][:, t, :],
                    in0=d_rows[t][:].indirect(entries(n2_l, HALVES[u])),
                    in1=d_tanh[:, t, HALVES[u]],
                    op=ALU.mult,
                )
        quantise_z(0)
        quantise_w2(0)
        quantise_z(1)

        last = PACK - 1
        out_rows = out.rearrange("(p t) c -> t p c", t=PACK)
        h_rows = [placed("h_rows%d" % t, [P, S], F32, H_AT + H_STEP * t) for t in range(PACK)]
        pa = [placed("pa%d" % t, [P, W], F32, PAIRS_AT + 2 * PAIR * t) for t in range(PACK)]
        pb = [placed("pb%d" % t, [P, W], F32, PAIRS_AT + 2 * PAIR * t + PAIR) for t in range(PACK)]
        a_less_b = [placed("a_less_b0", [P, W], F32, PAIRS_AT + 2 * PAIR + PAIR // 2)]
        a_less_b.extend(tile("a_less_b%d" % t, [P, W], F32) for t in range(1, PACK))
        sig_a = [tile("sig_a%d" % t, [P, W], F32) for t in range(PACK)]
        sig_b = [placed("sig_b%d" % t, [P, W], F32, H_AT + H_STEP * (t + 1) + LINE) for t in range(last)]
        sig_b.append(tile("sig_b%d" % last, [P, W], F32))
        res = [tile("res%d" % t, [P, S], F32) for t in range(PACK)]

        def multiply_h(t, b, cols):
            acc = bank(b, cols.stop - cols.start)
            plane = slice(t % 2 * P, (t % 2 + 1) * P)
            multiply(acc[:], w2_codes[t // 2][:, plane], w2_scales[t // 2][:, plane], z_codes[:, cols], z_scales[:, cols])
            nc.scalar.copy(out=h_rows[t][:, cols], in_=acc[:])

        def fetch_pairs(t):
            if t == 0:
                nc.vector.tensor_copy(out=pa[t][:], in_=h_rows[t][:].indirect(n3_l[:]))
            else:
                nc.scalar.activation(out=pa[t][:], in_=h_rows[t][:].indirect(n3_l[:]), func=ACT.Copy)
            nc.scalar.activation(out=pb[t][:], in_=h_rows[t][:].indirect(n4_l[:]), func=ACT.Copy)
            nc.vector.tensor_tensor(out=a_less_b[t][:], in0=pa[t][:], in1=pb[t][:], op=ALU.subtract)

        multiply_h(0, 0, HALVES[0])
        round_w2(1)
        multiply_h(0, 1, HALVES[1])
        quantise_w2(1)
        fetch_pairs(0)
        b_less_a0 = tile("b_less_a0", [P, W], F32)
        nc.vector.tensor_tensor(out=b_less_a0[:], in0=pb[0][:], in1=pa[0][:], op=ALU.subtract)
        for t in range(PACK):
            nc.scalar.activation(out=sig_a[t][:], in_=a_less_b[t][:], func=ACT.Sigmoid)
            nc.vector.tensor_tensor(out=res[t][:].indirect(n3_l[:]), in0=pa[t][:], in1=sig_a[t][:], op=ALU.mult)
            if t < last:
                multiply_h(t + 1, 2 + t, slice(0, S))
                fetch_pairs(t + 1)
            if t == 0:
                nc.scalar.activation(out=sig_b[t][:], in_=b_less_a0[:], func=ACT.Sigmoid)
            else:
                nc.scalar.activation(out=sig_b[t][:], in_=a_less_b[t][:], func=ACT.Sigmoid, scale=-1.0)
            nc.vector.tensor_tensor(out=res[t][:].indirect(n4_l[:]), in0=pb[t][:], in1=sig_b[t][:], op=ALU.mult)
            nc.sync.dma_start(out=out_rows[t], in_=res[t][:])
